import numpy as np
import ml_dtypes


def mxq(x, axis, fmt="e4m3"):
    dtype, down = {"e4m3": (ml_dtypes.float8_e4m3fn, 7), "e5m2": (ml_dtypes.float8_e5m2, 14)}[fmt]
    v = np.moveaxis(np.asarray(x, np.float32).astype(ml_dtypes.bfloat16).astype(np.float64), axis, -1)
    blocks = v.reshape(v.shape[:-1] + (-1, 32))
    amax = np.abs(blocks).max(-1, keepdims=True)
    byte = np.maximum(np.where(amax > 0, np.frexp(amax)[1] - 1 + 127, 0) - down, 1)
    scale = np.exp2(byte - 127.0)
    codes = (blocks / scale).astype(np.float32).astype(dtype).astype(np.float64)
    return np.moveaxis((codes * scale).reshape(v.shape), -1, axis)


WIDE = False


def mx_kscale(k):
    if not WIDE:
        return np.ones(k)
    levels = np.array([30, -30])
    if k % 512:
        return np.exp2(np.random.permutation(np.resize(levels, k // 32))).repeat(32)
    a = np.empty((k // 512, 16))
    for p in range(k // 512):
        a[p, :8] = np.random.permutation(np.resize(levels, 8))
        for g in range(8):
            far = levels[np.abs(levels - a[p, g]) >= 10]
            a[p, g + 8] = far[np.random.randint(len(far))]
    return np.exp2(a.ravel()).repeat(32)


def f64(x):
    return np.asarray(x).astype(np.float64)


def striped(idx):
    return np.tile(np.asarray(idx).reshape(-1, 16).T, (8, 1)).astype(np.uint16)


def unstriped(offs):
    return offs[:16].T.reshape(-1).astype(np.int64)


E2M1 = np.array([0.0, 0.5, 1.0, 1.5, 2.0, 3.0, 4.0, 6.0, -0.0, -0.5, -1.0, -1.5, -2.0, -3.0, -4.0, -6.0])


def pack_weight(w, fmt):
    k, n = w.shape
    w = f64(np.asarray(w, np.float32).astype(ml_dtypes.bfloat16)).reshape(k // 32, 32, n)
    amax = np.abs(w).max(1)
    if fmt in ("e4m3", "e5m2"):
        byte = np.frexp(amax)[1] - 1 + 127 - (7 if fmt == "e4m3" else 14)
    else:
        mant, ex = np.frexp(amax / 6.0)
        byte = np.where(mant > 0.5, ex, ex - 1) + 127
    byte = np.clip(np.where(amax > 0, byte, 1), 1, 254)
    scaled = (w * np.exp2(127.0 - byte)[:, None, :]).reshape(k, n).astype(np.float32)
    by_word = np.ascontiguousarray(scaled.reshape(k // 512, 128, 4, n).transpose(0, 1, 3, 2))
    if fmt in ("e4m3", "e5m2"):
        words = by_word.astype(ml_dtypes.float8_e4m3fn if fmt == "e4m3" else ml_dtypes.float8_e5m2).view(np.uint8)
    else:
        c = by_word.astype(ml_dtypes.float4_e2m1fn).view(np.uint8) & 0xF
        words = (c[..., 0::2] | (c[..., 1::2] << 4)).reshape(k // 512, 128, 2 * n)
    return np.ascontiguousarray(words), np.ascontiguousarray(byte.astype(np.uint8).reshape(k // 512, 16, n))


def unpack_weight(words, scales, fmt):
    g, _, n = scales.shape
    words = np.ascontiguousarray(words).reshape(g, 128, n, -1)
    if fmt in ("e4m3", "e5m2"):
        vals = words.view(ml_dtypes.float8_e4m3fn if fmt == "e4m3" else ml_dtypes.float8_e5m2).astype(np.float64)
    else:
        nib = np.empty((g, 128, n, 4), np.uint8)
        nib[..., 0::2] = words & 0xF
        nib[..., 1::2] = words >> 4
        vals = E2M1[nib]
    vals = vals * np.repeat(np.exp2(scales.astype(np.float64) - 127.0), 8, axis=1)[..., None]
    return vals.transpose(0, 1, 3, 2).reshape(g * 512, n)


K, T, J, R, N = 512, 2048, 256, 512, 256


def setup_inputs():
    n = np.random.standard_normal
    idx = np.random.permutation(T)[:J]
    idx2 = np.random.permutation(T)[:J]
    idx3 = np.random.permutation(T)[:J]
    idx4 = np.random.permutation(J)[:J]
    idx5 = np.random.permutation(J)[:J]
    fk = mx_kscale(K)
    fr = mx_kscale(R)
    xtp = pack_weight(n((K, T)) / fk[:, None], "e5m2")
    wp = pack_weight(n((K, R)) * 1 / np.sqrt(K) * fk[:, None] * fr, "e2m1")
    wbp = pack_weight(n((R, N)) * 1 / np.sqrt(R) / fr[:, None], "e2m1")
    wsp = pack_weight(n((K, N)) * 1 / np.sqrt(K) * fk[:, None], "e2m1")
    return {
        "xt_words": xtp[0],
        "xt_scales": xtp[1],
        "w_words": wp[0],
        "w_scales": wp[1],
        "wb_words": wbp[0],
        "wb_scales": wbp[1],
        "ws_words": wsp[0],
        "ws_scales": wsp[1],
        "offs": striped(idx),
        "offs2": striped(idx2),
        "offs3": striped(idx3),
        "offs4": striped(idx4),
        "offs5": striped(idx5),
    }


def reference(xt_words, xt_scales, w_words, w_scales, wb_words, wb_scales, ws_words, ws_scales, offs, offs2, offs3, offs4, offs5):
    idx = unstriped(offs)
    idx2 = unstriped(offs2)
    idx3 = unstriped(offs3)
    idx4 = unstriped(offs4)
    idx5 = unstriped(offs5)
    xtu = unpack_weight(xt_words, xt_scales, "e5m2")
    wu = unpack_weight(w_words, w_scales, "e2m1")
    wbu = unpack_weight(wb_words, wb_scales, "e2m1")
    wsu = unpack_weight(ws_words, ws_scales, "e2m1")
    xtidxg = xtu[:, idx]
    a = wu.T @ xtidxg
    xtidx2g = xtu[:, idx2]
    b = wu.T @ xtidx2g
    xtidx3g = xtu[:, idx3]
    g0 = wu.T @ xtidx3g
    hid = np.abs(np.maximum(a, b[:, idx4]) - g0[:, idx5])
    hidq = mxq(hid, 0, "e4m3")
    y = wbu.T @ hidq + wsu.T @ xtidxg
    return y

@@ -1,0 +1,223 @@
+from contextlib import ExitStack
+
+import concourse.mybir as mybir
+
+K, T, J, R, N = 512, 2048, 256, 512, 256
+FLOPS = 2 * K * R * J * 3 + 2 * R * N * J + 2 * K * N * J
+
+F32 = mybir.dt.float32
+BF16 = mybir.dt.bfloat16
+I32 = mybir.dt.int32
+U32 = mybir.dt.uint32
+U16 = mybir.dt.uint16
+U8 = mybir.dt.uint8
+E4M3 = mybir.dt.float8_e4m3fn_x4
+E5M2 = mybir.dt.float8_e5m2_x4
+E2M1 = mybir.dt.float4_e2m1fn_x4
+ALU = mybir.AluOpType
+ACT = mybir.ActivationFunctionType
+
+P = 128
+PACK = 4
+HALF = J // 2
+
+
+def load_scales(queues, plane, scales):
+    rows = scales[0].bitcast(I32)
+    for q in range(4):
+        queues[q].dma_start(out=plane[32 * q : 32 * q + 4, :].bitcast(I32), in_=rows[4 * q : 4 * q + 4, :])
+
+
+def tile_list_lessthird_triple_skip_plain_kernel(
+    tc, xt_words, xt_scales, w_words, w_scales, wb_words, wb_scales, ws_words, ws_scales,
+    offs, offs2, offs3, offs4, offs5, out,
+):
+    nc = tc.nc
+    with ExitStack() as ctx:
+        keep = ctx.enter_context(tc.tile_pool(name="keep", bufs=1))
+        psum = ctx.enter_context(tc.psum_pool(name="psum", bufs=1))
+
+        def sb(name, shape, dtype):
+            return keep.tile(shape, dtype, name=name, align_bytes=64)
+
+        def load_list(name, src):
+            tile = keep.tile([P, J // 16], U16, name=name)
+            nc.sync.dma_start(tile[:], src)
+            return tile
+
+        on_sync = [nc.sync] * 4
+        on_both = [nc.sync, nc.scalar, nc.sync, nc.scalar]
+        x_words = sb("x_words", [P, T], U32)
+        w_raw = sb("w_raw", [P, 2 * R], U8)
+        nc.gpsimd.dma_start(out=w_raw[:].bitcast(I32), in_=w_words[0].bitcast(I32))
+        x_scales = sb("x_scales", [P, T], U8)
+        w_raw_scales = sb("w_raw_scales", [P, R], U8)
+        ws_plane = sb("ws_plane", [P, N], U8)
+        wb_plane = sb("wb_plane", [P, N], U8)
+        for plane in (x_scales, w_raw_scales, ws_plane, wb_plane):
+            nc.vector.memset(plane[:].bitcast(I32), 0)
+        list_b = load_list("list_b", offs2)
+        list_a = load_list("list_a", offs)
+        list_g = load_list("list_g", offs3)
+        load_scales(on_both, x_scales, xt_scales)
+        nc.sync.dma_start(out=x_words[:].bitcast(I32), in_=xt_words[0].rearrange("p n t -> p (n t)").bitcast(I32))
+        load_scales(on_sync, w_raw_scales, w_scales)
+        pick_b = load_list("pick_b", offs4)
+        pick_g = load_list("pick_g", offs5)
+        ws_codes = sb("ws_codes", [P, 2 * N], U8)
+        nc.sync.dma_start(out=ws_codes[:].bitcast(I32), in_=ws_words[0].bitcast(I32))
+        load_scales(on_sync, ws_plane, ws_scales)
+        wb_codes = sb("wb_codes", [P, 2 * N], U8)
+        nc.sync.dma_start(out=wb_codes[:].bitcast(I32), in_=wb_words[0].bitcast(I32))
+        load_scales(on_sync, wb_plane, wb_scales)
+
+        w_codes = sb("w_codes", [P, 2 * R], U8)
+        nc.scalar.copy(
+            out=w_codes[:].bitcast(U16).rearrange("p (t m) -> p t m", t=PACK),
+            in_=w_raw[:].bitcast(U16).rearrange("p (m t) -> p t m", t=PACK),
+        )
+        w_plane = sb("w_plane", [P, R], U8)
+        for u in range(2):
+            nc.gpsimd.tensor_copy(
+                out=w_plane[:].rearrange("p (t m) -> p t m", t=PACK)[:, 2 * u : 2 * u + 2, :],
+                in_=w_raw_scales[:].rearrange("p (m t) -> p t m", t=PACK)[:, 2 * u : 2 * u + 2, :],
+            )
+
+        lists = {"b": list_b, "a": list_a, "g": list_g}
+        tok_scales, tok_words = {}, {}
+        for name in ("b", "a", "g"):
+            tok_scales[name] = sb("tok_scales_" + name, [P, J], U8)
+            nc.vector.tensor_copy(out=tok_scales[name][:], in_=x_scales[:].indirect(lists[name][:]))
+        for name in ("b", "a", "g"):
+            tok_words[name] = sb("tok_words_" + name, [P, J], U32)
+            nc.vector.tensor_copy(out=tok_words[name][:], in_=x_words[:].indirect(lists[name][:]))
+
+        def first_product(dst, name, t):
+            nc.tensor.matmul_mx(
+                out=dst,
+                lhsT=w_codes[:, 2 * P * t : 2 * P * (t + 1)].bitcast(E2M1),
+                lhsT_scale=w_plane[:, P * t : P * (t + 1)],
+                rhs=tok_words[name][:].bitcast(E5M2),
+                rhs_scale=tok_scales[name][:],
+                start=True,
+                stop=True,
+            )
+
+        def bank(name, tag, shape):
+            return psum.tile(shape, F32, name=name, tag=tag)
+
+        bg_banks = [bank("bg_bank%d" % t, "bank%d" % t, [P, 2, J]) for t in range(PACK)]
+        a_banks = [bank("a_bank%d" % u, "bank%d" % (4 + u), [P, 2, J]) for u in range(2)]
+        b_sb = [sb("b_sb%d" % t, [P, J], F32) for t in range(PACK)]
+        g_sb = [sb("g_sb%d" % t, [P, J], F32) for t in range(PACK)]
+        picked = [sb("picked%d" % h, [P, PACK, HALF], F32) for h in range(2)]
+        larger = [sb("larger%d" % h, [P, PACK, HALF], F32) for h in range(2)]
+        diff = [sb("diff%d" % h, [P, PACK, HALF], F32) for h in range(2)]
+        hid = [sb("hid%d" % h, [P, HALF, PACK], BF16) for h in range(2)]
+        hid_codes = [sb("hid_codes%d" % h, [P, HALF], U32) for h in range(2)]
+        hid_plane = [sb("hid_plane%d" % h, [P, HALF], U8) for h in range(2)]
+        cols = [slice(h * HALF, (h + 1) * HALF) for h in range(2)]
+
+        def entries(tile, h):
+            return tile[:, h * HALF // 16 : (h + 1) * HALF // 16]
+
+        def pick_b_columns(t, h, on_vector):
+            window = b_sb[t][:].indirect(entries(pick_b, h))
+            if on_vector:
+                nc.vector.tensor_copy(out=picked[h][:, t, :], in_=window)
+            else:
+                nc.scalar.activation(out=picked[h][:, t, :], in_=window, func=ACT.Copy)
+
+        def take_larger(u, h):
+            nc.vector.tensor_tensor(
+                out=larger[h][:, 2 * u : 2 * u + 2, :], in0=a_banks[u][:, :, cols[h]],
+                in1=picked[h][:, 2 * u : 2 * u + 2, :], op=ALU.max,
+            )
+
+        def subtract(t, h):
+            nc.vector.tensor_tensor(
+                out=diff[h][:, t, :], in0=g_sb[t][:].indirect(entries(pick_g, h)),
+                in1=larger[h][:, t, :], op=ALU.subtract,
+            )
+
+        def magnitude(h, slots):
+            nc.scalar.activation(
+                out=hid[h][:].rearrange("p (c i) t -> p c t i", i=4)[:, :, slots, :],
+                in_=diff[h][:].rearrange("p t (c i) -> p c t i", i=4)[:, :, slots, :],
+                func=ACT.Abs,
+            )
+
+        def quantise(h):
+            nc.vector.quantize_mx(
+                out=hid_codes[h][:].bitcast(E4M3), scales=hid_plane[h][:],
+                in_=hid[h][:].rearrange("p j t -> p (j t)"),
+            )
+
+        def second_pass(dst, n, codes, plane, rhs, rhs_scale, start, stop):
+            nc.tensor.matmul_mx(
+                out=dst,
+                lhsT=codes[:, 2 * P * n : 2 * P * (n + 1)].bitcast(E2M1),
+                lhsT_scale=plane[:, P * n : P * (n + 1)],
+                rhs=rhs,
+                rhs_scale=rhs_scale,
+                start=start,
+                stop=stop,
+            )
+
+        def short_way(dst, h, n, start):
+            second_pass(dst, n, ws_codes, ws_plane, tok_words["a"][:, cols[h]].bitcast(E5M2),
+                        tok_scales["a"][:, cols[h]], start, False)
+
+        def output_product(dst, h, n, stop):
+            second_pass(dst, n, wb_codes, wb_plane, hid_codes[h][:].bitcast(E4M3), hid_plane[h][:], False, stop)
+
+        for u in range(2):
+            pair = (2 * u, 2 * u + 1)
+            halves = (1, 0) if u == 0 else (0, 1)
+            for t in pair:
+                first_product(bg_banks[t][:, 0, :], "b", t)
+                if t == 1:
+                    nc.vector.tensor_copy(out=b_sb[t][:], in_=bg_banks[t][:, 0, :])
+                else:
+                    nc.scalar.copy(out=b_sb[t][:], in_=bg_banks[t][:, 0, :])
+            for t in pair:
+                first_product(a_banks[u][:, t % 2, :], "a", t)
+            for t in pair:
+                first_product(bg_banks[t][:, 1, :], "g", t)
+            for h in range(2):
+                for t in pair:
+                    pick_b_columns(t, h, on_vector=(u == 0 and h == 0))
+            for t in pair:
+                nc.scalar.copy(out=g_sb[t][:], in_=bg_banks[t][:, 1, :])
+            for h in halves:
+                take_larger(u, h)
+            for h in halves:
+                for t in pair:
+                    subtract(t, h)
+
+        y0_bank = bank("y0_bank", "bank6", [P, 2, HALF])
+        y1_banks = [bank("y1_bank0", "bank7", [P, HALF]), bank("y1_bank1", "bank0", [P, HALF])]
+        for n in range(2):
+            short_way(y0_bank[:, n, :], 0, n, n == 0)
+        for n in range(2):
+            short_way(y1_banks[n][:], 1, n, True)
+
+        magnitude(1, slice(0, 2))
+        magnitude(0, slice(0, 4))
+        magnitude(1, slice(2, 4))
+        quantise(0)
+        quantise(1)
+        for n in range(2):
+            output_product(y0_bank[:, n, :], 0, n, n == 1)
+        for n in range(2):
+            output_product(y1_banks[n][:], 1, n, True)
+
+        out_view = out.rearrange("(n p) j -> p n j", p=P)
+        y0 = sb("y0", [P, 2, HALF], F32)
+        nc.scalar.copy(out=y0[:], in_=y0_bank[:])
+        nc.sync.dma_start(out=out_view[:, :, cols[0]], in_=y0[:])
+        y1 = [sb("y1_%d" % n, [P, HALF], F32) for n in range(2)]
+        nc.vector.tensor_copy(out=y1[0][:], in_=y1_banks[0][:])
+        nc.sync.dma_start(out=out_view[:, 0, cols[1]], in_=y1[0][:])
+        nc.scalar.copy(out=y1[1][:], in_=y1_banks[1][:])
+        nc.scalar.dma_start(out=out_view[:, 1, cols[1]], in_=y1[1][:])

@@ -49,18 +49,21 @@ def tile_list_lessthird_triple_skip_plain_kernel(
         on_both = [nc.sync, nc.scalar, nc.sync, nc.scalar]
         x_words = sb("x_words", [P, T], U32)
         w_raw = sb("w_raw", [P, 2 * R], U8)
-        nc.gpsimd.dma_start(out=w_raw[:].bitcast(I32), in_=w_words[0].bitcast(I32))
         x_scales = sb("x_scales", [P, T], U8)
         w_raw_scales = sb("w_raw_scales", [P, R], U8)
         ws_plane = sb("ws_plane", [P, N], U8)
         wb_plane = sb("wb_plane", [P, N], U8)
         for plane in (x_scales, w_raw_scales, ws_plane, wb_plane):
             nc.vector.memset(plane[:].bitcast(I32), 0)
+        windows = [sb("window%d" % t, [P, 3, J], F32) for t in range(PACK)]
+        for window in windows:
+            nc.vector.memset(window[:, 2, :], 0.0)
         list_b = load_list("list_b", offs2)
         list_a = load_list("list_a", offs)
         list_g = load_list("list_g", offs3)
         load_scales(on_both, x_scales, xt_scales)
         nc.sync.dma_start(out=x_words[:].bitcast(I32), in_=xt_words[0].rearrange("p n t -> p (n t)").bitcast(I32))
+        nc.sync.dma_start(out=w_raw[:].bitcast(I32), in_=w_words[0].bitcast(I32))
         load_scales(on_sync, w_raw_scales, w_scales)
         pick_b = load_list("pick_b", offs4)
         pick_g = load_list("pick_g", offs5)
@@ -84,20 +87,21 @@ def tile_list_lessthird_triple_skip_plain_kernel(
             )
 
         lists = {"b": list_b, "a": list_a, "g": list_g}
-        tok_scales, tok_words = {}, {}
+        tok_scales = {}
         for name in ("b", "a", "g"):
             tok_scales[name] = sb("tok_scales_" + name, [P, J], U8)
             nc.vector.tensor_copy(out=tok_scales[name][:], in_=x_scales[:].indirect(lists[name][:]))
+        tok_words = {}
         for name in ("b", "a", "g"):
-            tok_words[name] = sb("tok_words_" + name, [P, J], U32)
-            nc.vector.tensor_copy(out=tok_words[name][:], in_=x_words[:].indirect(lists[name][:]))
+            tok_words[name] = sb("tok_words_" + name, [P, J], U32)[:]
+            nc.vector.tensor_copy(out=tok_words[name], in_=x_words[:].indirect(lists[name][:]))
 
         def first_product(dst, name, t):
             nc.tensor.matmul_mx(
                 out=dst,
                 lhsT=w_codes[:, 2 * P * t : 2 * P * (t + 1)].bitcast(E2M1),
                 lhsT_scale=w_plane[:, P * t : P * (t + 1)],
-                rhs=tok_words[name][:].bitcast(E5M2),
+                rhs=tok_words[name].bitcast(E5M2),
                 rhs_scale=tok_scales[name][:],
                 start=True,
                 stop=True,
@@ -106,51 +110,63 @@ def tile_list_lessthird_triple_skip_plain_kernel(
         def bank(name, tag, shape):
             return psum.tile(shape, F32, name=name, tag=tag)
 
-        bg_banks = [bank("bg_bank%d" % t, "bank%d" % t, [P, 2, J]) for t in range(PACK)]
-        a_banks = [bank("a_bank%d" % u, "bank%d" % (4 + u), [P, 2, J]) for u in range(2)]
-        b_sb = [sb("b_sb%d" % t, [P, J], F32) for t in range(PACK)]
-        g_sb = [sb("g_sb%d" % t, [P, J], F32) for t in range(PACK)]
-        picked = [sb("picked%d" % h, [P, PACK, HALF], F32) for h in range(2)]
-        larger = [sb("larger%d" % h, [P, PACK, HALF], F32) for h in range(2)]
-        diff = [sb("diff%d" % h, [P, PACK, HALF], F32) for h in range(2)]
-        hid = [sb("hid%d" % h, [P, HALF, PACK], BF16) for h in range(2)]
+        bg0, bg1, bg3 = [bank("bg%d" % t, "bank%d" % t, [P, 2, J]) for t in (0, 1, 3)]
+        b2 = bank("b2", "bank2", [P, J])
+        g2 = bank("g2", "bank5", [P, J])
+        a01 = bank("a01", "bank4", [P, 2, J])
+        a23 = bank("a23", "bank2", [P, 2, J])
+        b_psum = [bg0[:, 0, :], bg1[:, 0, :], b2[:], bg3[:, 0, :]]
+        g_psum = [bg0[:, 1, :], bg1[:, 1, :], g2[:], bg3[:, 1, :]]
+        a_psum = [a01[:, 0, :], a01[:, 1, :], a23[:, 0, :], a23[:, 1, :]]
+        picked = sb("picked", [P, PACK, J], F32)
+        larger = sb("larger", [P, PACK, J], F32)
+        diff = sb("diff", [P, PACK, J], F32)
+        hid = sb("hid", [P, J, PACK], BF16)
         hid_codes = [sb("hid_codes%d" % h, [P, HALF], U32) for h in range(2)]
         hid_plane = [sb("hid_plane%d" % h, [P, HALF], U8) for h in range(2)]
         cols = [slice(h * HALF, (h + 1) * HALF) for h in range(2)]
+        every = slice(0, J)
 
-        def entries(tile, h):
-            return tile[:, h * HALF // 16 : (h + 1) * HALF // 16]
+        def entries(tile, span):
+            return tile[:, span.start // 16 : span.stop // 16]
 
-        def pick_b_columns(t, h, on_vector):
-            window = b_sb[t][:].indirect(entries(pick_b, h))
+        def copy_b(t, on_vector):
             if on_vector:
-                nc.vector.tensor_copy(out=picked[h][:, t, :], in_=window)
+                nc.vector.tensor_copy(out=windows[t][:, 1, :], in_=b_psum[t])
             else:
-                nc.scalar.activation(out=picked[h][:, t, :], in_=window, func=ACT.Copy)
+                nc.scalar.copy(out=windows[t][:, 1, :], in_=b_psum[t])
 
-        def take_larger(u, h):
+        def copy_g(t):
+            nc.scalar.copy(out=windows[t][:, 0, :], in_=g_psum[t])
+
+        def pick_b_columns(t, on_vector):
+            window = windows[t][:].rearrange("p s j -> p (s j)")[:, J:].indirect(pick_b[:])
+            if on_vector:
+                nc.vector.tensor_copy(out=picked[:, t, :], in_=window)
+            else:
+                nc.scalar.activation(out=picked[:, t, :], in_=window, func=ACT.Copy)
+
+        def take_larger(t):
+            nc.vector.tensor_tensor(out=larger[:, t, :], in0=a_psum[t], in1=picked[:, t, :], op=ALU.max)
+
+        def subtract(t, span):
             nc.vector.tensor_tensor(
-                out=larger[h][:, 2 * u : 2 * u + 2, :], in0=a_banks[u][:, :, cols[h]],
-                in1=picked[h][:, 2 * u : 2 * u + 2, :], op=ALU.max,
+                out=diff[:, t, span],
+                in0=windows[t][:].rearrange("p s j -> p (s j)").indirect(entries(pick_g, span)),
+                in1=larger[:, t, span], op=ALU.subtract,
             )
 
-        def subtract(t, h):
-            nc.vector.tensor_tensor(
-                out=diff[h][:, t, :], in0=g_sb[t][:].indirect(entries(pick_g, h)),
-                in1=larger[h][:, t, :], op=ALU.subtract,
-            )
-
-        def magnitude(h, slots):
+        def magnitude(span):
             nc.scalar.activation(
-                out=hid[h][:].rearrange("p (c i) t -> p c t i", i=4)[:, :, slots, :],
-                in_=diff[h][:].rearrange("p t (c i) -> p c t i", i=4)[:, :, slots, :],
+                out=hid[:, span, :].rearrange("p (c i) t -> p c t i", i=4),
+                in_=diff[:, :, span].rearrange("p t (c i) -> p c t i", i=4),
                 func=ACT.Abs,
             )
 
         def quantise(h):
             nc.vector.quantize_mx(
                 out=hid_codes[h][:].bitcast(E4M3), scales=hid_plane[h][:],
-                in_=hid[h][:].rearrange("p j t -> p (j t)"),
+                in_=hid[:, cols[h], :].rearrange("p j t -> p (j t)"),
             )
 
         def second_pass(dst, n, codes, plane, rhs, rhs_scale, start, stop):
@@ -171,29 +187,36 @@ def tile_list_lessthird_triple_skip_plain_kernel(
         def output_product(dst, h, n, stop):
             second_pass(dst, n, wb_codes, wb_plane, hid_codes[h][:].bitcast(E4M3), hid_plane[h][:], False, stop)
 
-        for u in range(2):
-            pair = (2 * u, 2 * u + 1)
-            halves = (1, 0) if u == 0 else (0, 1)
-            for t in pair:
-                first_product(bg_banks[t][:, 0, :], "b", t)
-                if t == 1:
-                    nc.vector.tensor_copy(out=b_sb[t][:], in_=bg_banks[t][:, 0, :])
-                else:
-                    nc.scalar.copy(out=b_sb[t][:], in_=bg_banks[t][:, 0, :])
-            for t in pair:
-                first_product(a_banks[u][:, t % 2, :], "a", t)
-            for t in pair:
-                first_product(bg_banks[t][:, 1, :], "g", t)
-            for h in range(2):
-                for t in pair:
-                    pick_b_columns(t, h, on_vector=(u == 0 and h == 0))
-            for t in pair:
-                nc.scalar.copy(out=g_sb[t][:], in_=bg_banks[t][:, 1, :])
-            for h in halves:
-                take_larger(u, h)
-            for h in halves:
-                for t in pair:
-                    subtract(t, h)
+        for t in range(PACK):
+            first_product(b_psum[t], "b", t)
+        for t in range(3):
+            copy_b(t, on_vector=(t == 2))
+        pick_b_columns(0, on_vector=False)
+        pick_b_columns(1, on_vector=True)
+        copy_b(3, on_vector=False)
+        for t in range(2):
+            first_product(a_psum[t], "a", t)
+        for t in range(2):
+            first_product(g_psum[t], "g", t)
+        for t in range(2, 4):
+            first_product(a_psum[t], "a", t)
+            first_product(g_psum[t], "g", t)
+
+        copy_g(0)
+        copy_g(1)
+        pick_b_columns(2, on_vector=False)
+        pick_b_columns(3, on_vector=False)
+        copy_g(2)
+        copy_g(3)
+        take_larger(0)
+        take_larger(1)
+        subtract(0, every)
+        subtract(1, every)
+        take_larger(2)
+        take_larger(3)
+        for h in range(2):
+            subtract(2, cols[h])
+            subtract(3, cols[h])
 
         y0_bank = bank("y0_bank", "bank6", [P, 2, HALF])
         y1_banks = [bank("y1_bank0", "bank7", [P, HALF]), bank("y1_bank1", "bank0", [P, HALF])]
@@ -202,9 +225,8 @@ def tile_list_lessthird_triple_skip_plain_kernel(
         for n in range(2):
             short_way(y1_banks[n][:], 1, n, True)
 
-        magnitude(1, slice(0, 2))
-        magnitude(0, slice(0, 4))
-        magnitude(1, slice(2, 4))
+        magnitude(cols[0])
+        magnitude(cols[1])
         quantise(0)
         quantise(1)
         for n in range(2):

from contextlib import ExitStack

import concourse.mybir as mybir

K, T, J, R, N = 512, 2048, 256, 512, 256
FLOPS = 2 * K * R * J * 3 + 2 * R * N * J + 2 * K * N * J

F32 = mybir.dt.float32
BF16 = mybir.dt.bfloat16
I32 = mybir.dt.int32
U32 = mybir.dt.uint32
U16 = mybir.dt.uint16
U8 = mybir.dt.uint8
E4M3 = mybir.dt.float8_e4m3fn_x4
E5M2 = mybir.dt.float8_e5m2_x4
E2M1 = mybir.dt.float4_e2m1fn_x4
ALU = mybir.AluOpType
ACT = mybir.ActivationFunctionType

P = 128
PACK = 4
HALF = J // 2


def load_scales(queues, plane, scales):
    rows = scales[0].bitcast(I32)
    for q in range(4):
        queues[q].dma_start(out=plane[32 * q : 32 * q + 4, :].bitcast(I32), in_=rows[4 * q : 4 * q + 4, :])


def tile_list_lessthird_triple_skip_plain_kernel(
    tc, xt_words, xt_scales, w_words, w_scales, wb_words, wb_scales, ws_words, ws_scales,
    offs, offs2, offs3, offs4, offs5, out,
):
    nc = tc.nc
    with ExitStack() as ctx:
        keep = ctx.enter_context(tc.tile_pool(name="keep", bufs=1))
        psum = ctx.enter_context(tc.psum_pool(name="psum", bufs=1))

        def sb(name, shape, dtype):
            return keep.tile(shape, dtype, name=name, align_bytes=64)

        def load_list(name, src):
            tile = keep.tile([P, J // 16], U16, name=name)
            nc.sync.dma_start(tile[:], src)
            return tile

        on_sync = [nc.sync] * 4
        on_both = [nc.sync, nc.scalar, nc.sync, nc.scalar]
        x_words = sb("x_words", [P, T], U32)
        w_raw = sb("w_raw", [P, 2 * R], U8)
        x_scales = sb("x_scales", [P, T], U8)
        w_raw_scales = sb("w_raw_scales", [P, R], U8)
        ws_plane = sb("ws_plane", [P, N], U8)
        wb_plane = sb("wb_plane", [P, N], U8)
        for plane in (x_scales, w_raw_scales, ws_plane, wb_plane):
            nc.vector.memset(plane[:].bitcast(I32), 0)
        windows = [sb("window%d" % t, [P, 3, J], F32) for t in range(PACK)]
        for window in windows:
            nc.vector.memset(window[:, 2, :], 0.0)
        list_b = load_list("list_b", offs2)
        list_a = load_list("list_a", offs)
        list_g = load_list("list_g", offs3)
        load_scales(on_both, x_scales, xt_scales)
        nc.sync.dma_start(out=x_words[:].bitcast(I32), in_=xt_words[0].rearrange("p n t -> p (n t)").bitcast(I32))
        nc.sync.dma_start(out=w_raw[:].bitcast(I32), in_=w_words[0].bitcast(I32))
        load_scales(on_sync, w_raw_scales, w_scales)
        pick_b = load_list("pick_b", offs4)
        pick_g = load_list("pick_g", offs5)
        ws_codes = sb("ws_codes", [P, 2 * N], U8)
        nc.sync.dma_start(out=ws_codes[:].bitcast(I32), in_=ws_words[0].bitcast(I32))
        load_scales(on_sync, ws_plane, ws_scales)
        wb_codes = sb("wb_codes", [P, 2 * N], U8)
        nc.sync.dma_start(out=wb_codes[:].bitcast(I32), in_=wb_words[0].bitcast(I32))
        load_scales(on_sync, wb_plane, wb_scales)

        w_codes = sb("w_codes", [P, 2 * R], U8)
        nc.scalar.copy(
            out=w_codes[:].bitcast(U16).rearrange("p (t m) -> p t m", t=PACK),
            in_=w_raw[:].bitcast(U16).rearrange("p (m t) -> p t m", t=PACK),
        )
        w_plane = sb("w_plane", [P, R], U8)
        for u in range(2):
            nc.gpsimd.tensor_copy(
                out=w_plane[:].rearrange("p (t m) -> p t m", t=PACK)[:, 2 * u : 2 * u + 2, :],
                in_=w_raw_scales[:].rearrange("p (m t) -> p t m", t=PACK)[:, 2 * u : 2 * u + 2, :],
            )

        lists = {"b": list_b, "a": list_a, "g": list_g}
        tok_scales = {}
        for name in ("b", "a", "g"):
            tok_scales[name] = sb("tok_scales_" + name, [P, J], U8)
            nc.vector.tensor_copy(out=tok_scales[name][:], in_=x_scales[:].indirect(lists[name][:]))
        tok_words = {}
        for name in ("b", "a", "g"):
            tok_words[name] = sb("tok_words_" + name, [P, J], U32)[:]
            nc.vector.tensor_copy(out=tok_words[name], in_=x_words[:].indirect(lists[name][:]))

        def first_product(dst, name, t):
            nc.tensor.matmul_mx(
                out=dst,
                lhsT=w_codes[:, 2 * P * t : 2 * P * (t + 1)].bitcast(E2M1),
                lhsT_scale=w_plane[:, P * t : P * (t + 1)],
                rhs=tok_words[name].bitcast(E5M2),
                rhs_scale=tok_scales[name][:],
                start=True,
                stop=True,
            )

        def bank(name, tag, shape):
            return psum.tile(shape, F32, name=name, tag=tag)

        bg0, bg1, bg3 = [bank("bg%d" % t, "bank%d" % t, [P, 2, J]) for t in (0, 1, 3)]
        b2 = bank("b2", "bank2", [P, J])
        g2 = bank("g2", "bank5", [P, J])
        a01 = bank("a01", "bank4", [P, 2, J])
        a23 = bank("a23", "bank2", [P, 2, J])
        b_psum = [bg0[:, 0, :], bg1[:, 0, :], b2[:], bg3[:, 0, :]]
        g_psum = [bg0[:, 1, :], bg1[:, 1, :], g2[:], bg3[:, 1, :]]
        a_psum = [a01[:, 0, :], a01[:, 1, :], a23[:, 0, :], a23[:, 1, :]]
        picked = sb("picked", [P, PACK, J], F32)
        larger = sb("larger", [P, PACK, J], F32)
        diff = sb("diff", [P, PACK, J], F32)
        hid = sb("hid", [P, J, PACK], BF16)
        hid_codes = [sb("hid_codes%d" % h, [P, HALF], U32) for h in range(2)]
        hid_plane = [sb("hid_plane%d" % h, [P, HALF], U8) for h in range(2)]
        cols = [slice(h * HALF, (h + 1) * HALF) for h in range(2)]
        every = slice(0, J)

        def entries(tile, span):
            return tile[:, span.start // 16 : span.stop // 16]

        def copy_b(t, on_vector):
            if on_vector:
                nc.vector.tensor_copy(out=windows[t][:, 1, :], in_=b_psum[t])
            else:
                nc.scalar.copy(out=windows[t][:, 1, :], in_=b_psum[t])

        def copy_g(t):
            nc.scalar.copy(out=windows[t][:, 0, :], in_=g_psum[t])

        def pick_b_columns(t, on_vector):
            window = windows[t][:].rearrange("p s j -> p (s j)")[:, J:].indirect(pick_b[:])
            if on_vector:
                nc.vector.tensor_copy(out=picked[:, t, :], in_=window)
            else:
                nc.scalar.activation(out=picked[:, t, :], in_=window, func=ACT.Copy)

        def take_larger(t):
            nc.vector.tensor_tensor(out=larger[:, t, :], in0=a_psum[t], in1=picked[:, t, :], op=ALU.max)

        def subtract(t, span):
            nc.vector.tensor_tensor(
                out=diff[:, t, span],
                in0=windows[t][:].rearrange("p s j -> p (s j)").indirect(entries(pick_g, span)),
                in1=larger[:, t, span], op=ALU.subtract,
            )

        def magnitude(span):
            nc.scalar.activation(
                out=hid[:, span, :].rearrange("p (c i) t -> p c t i", i=4),
                in_=diff[:, :, span].rearrange("p t (c i) -> p c t i", i=4),
                func=ACT.Abs,
            )

        def quantise(h):
            nc.vector.quantize_mx(
                out=hid_codes[h][:].bitcast(E4M3), scales=hid_plane[h][:],
                in_=hid[:, cols[h], :].rearrange("p j t -> p (j t)"),
            )

        def second_pass(dst, n, codes, plane, rhs, rhs_scale, start, stop):
            nc.tensor.matmul_mx(
                out=dst,
                lhsT=codes[:, 2 * P * n : 2 * P * (n + 1)].bitcast(E2M1),
                lhsT_scale=plane[:, P * n : P * (n + 1)],
                rhs=rhs,
                rhs_scale=rhs_scale,
                start=start,
                stop=stop,
            )

        def short_way(dst, h, n, start):
            second_pass(dst, n, ws_codes, ws_plane, tok_words["a"][:, cols[h]].bitcast(E5M2),
                        tok_scales["a"][:, cols[h]], start, False)

        def output_product(dst, h, n, stop):
            second_pass(dst, n, wb_codes, wb_plane, hid_codes[h][:].bitcast(E4M3), hid_plane[h][:], False, stop)

        for t in range(PACK):
            first_product(b_psum[t], "b", t)
        for t in range(3):
            copy_b(t, on_vector=(t == 2))
        pick_b_columns(0, on_vector=False)
        pick_b_columns(1, on_vector=True)
        copy_b(3, on_vector=False)
        for t in range(2):
            first_product(a_psum[t], "a", t)
        for t in range(2):
            first_product(g_psum[t], "g", t)
        for t in range(2, 4):
            first_product(a_psum[t], "a", t)
            first_product(g_psum[t], "g", t)

        copy_g(0)
        copy_g(1)
        pick_b_columns(2, on_vector=False)
        pick_b_columns(3, on_vector=False)
        copy_g(2)
        copy_g(3)
        take_larger(0)
        take_larger(1)
        subtract(0, every)
        subtract(1, every)
        take_larger(2)
        take_larger(3)
        for h in range(2):
            subtract(2, cols[h])
            subtract(3, cols[h])

        y0_bank = bank("y0_bank", "bank6", [P, 2, HALF])
        y1_banks = [bank("y1_bank0", "bank7", [P, HALF]), bank("y1_bank1", "bank0", [P, HALF])]
        for n in range(2):
            short_way(y0_bank[:, n, :], 0, n, n == 0)
        for n in range(2):
            short_way(y1_banks[n][:], 1, n, True)

        magnitude(cols[0])
        magnitude(cols[1])
        quantise(0)
        quantise(1)
        for n in range(2):
            output_product(y0_bank[:, n, :], 0, n, n == 1)
        for n in range(2):
            output_product(y1_banks[n][:], 1, n, True)

        out_view = out.rearrange("(n p) j -> p n j", p=P)
        y0 = sb("y0", [P, 2, HALF], F32)
        nc.scalar.copy(out=y0[:], in_=y0_bank[:])
        nc.sync.dma_start(out=out_view[:, :, cols[0]], in_=y0[:])
        y1 = [sb("y1_%d" % n, [P, HALF], F32) for n in range(2)]
        nc.vector.tensor_copy(out=y1[0][:], in_=y1_banks[0][:])
        nc.sync.dma_start(out=out_view[:, 0, cols[1]], in_=y1[0][:])
        nc.scalar.copy(out=y1[1][:], in_=y1_banks[1][:])
        nc.scalar.dma_start(out=out_view[:, 1, cols[1]], in_=y1[1][:])
